import numpy as np
import ml_dtypes


def mxq(x, axis, fmt="e4m3"):
    dtype, down = {"e4m3": (ml_dtypes.float8_e4m3fn, 7), "e5m2": (ml_dtypes.float8_e5m2, 14)}[fmt]
    v = np.moveaxis(np.asarray(x, np.float32).astype(ml_dtypes.bfloat16).astype(np.float64), axis, -1)
    blocks = v.reshape(v.shape[:-1] + (-1, 32))
    amax = np.abs(blocks).max(-1, keepdims=True)
    byte = np.maximum(np.where(amax > 0, np.frexp(amax)[1] - 1 + 127, 0) - down, 1)
    scale = np.exp2(byte - 127.0)
    codes = (blocks / scale).astype(np.float32).astype(dtype).astype(np.float64)
    return np.moveaxis((codes * scale).reshape(v.shape), -1, axis)


WIDE = False


def mx_kscale(k):
    if not WIDE:
        return np.ones(k)
    levels = np.array([10, -10, 5, -5, 0])
    if k % 512:
        return np.exp2(np.random.permutation(np.resize(levels, k // 32))).repeat(32)
    a = np.empty((k // 512, 16))
    for p in range(k // 512):
        a[p, :8] = np.random.permutation(np.resize(levels, 8))
        for g in range(8):
            far = levels[np.abs(levels - a[p, g]) >= 10]
            a[p, g + 8] = far[np.random.randint(len(far))]
    return np.exp2(a.ravel()).repeat(32)


BF16 = ml_dtypes.bfloat16


def bf(x):
    return np.asarray(x, np.float32).astype(BF16)


def f64(x):
    return np.asarray(x).astype(np.float64)


E2M1 = np.array([0.0, 0.5, 1.0, 1.5, 2.0, 3.0, 4.0, 6.0, -0.0, -0.5, -1.0, -1.5, -2.0, -3.0, -4.0, -6.0])


def pack_weight(w, fmt):
    k, n = w.shape
    w = f64(bf(w)).reshape(k // 32, 32, n)
    amax = np.abs(w).max(1)
    if fmt == "e4m3":
        byte = np.frexp(amax)[1] - 1 + 127 - 7
    else:
        mant, ex = np.frexp(amax / 6.0)
        byte = np.where(mant > 0.5, ex, ex - 1) + 127
    byte = np.clip(np.where(amax > 0, byte, 1), 1, 254)
    scaled = (w * np.exp2(127.0 - byte)[:, None, :]).reshape(k, n).astype(np.float32)
    by_word = np.ascontiguousarray(scaled.reshape(k // 512, 128, 4, n).transpose(0, 1, 3, 2))
    if fmt == "e4m3":
        words = by_word.astype(ml_dtypes.float8_e4m3fn).view(np.uint8)
    else:
        c = by_word.astype(ml_dtypes.float4_e2m1fn).view(np.uint8) & 0xF
        words = c[..., 0::2] | (c[..., 1::2] << 4)
    return np.ascontiguousarray(words), np.ascontiguousarray(byte.astype(np.uint8).reshape(k // 512, 16, n))


def unpack_weight(words, scales, fmt):
    g, p, n, _ = words.shape
    if fmt == "e4m3":
        vals = np.ascontiguousarray(words).view(ml_dtypes.float8_e4m3fn).astype(np.float64)
    else:
        nib = np.empty((g, p, n, 4), np.uint8)
        nib[..., 0::2] = words & 0xF
        nib[..., 1::2] = words >> 4
        vals = E2M1[nib]
    vals = vals * np.repeat(np.exp2(scales.astype(np.float64) - 127.0), 8, axis=1)[..., None]
    return vals.transpose(0, 1, 3, 2).reshape(g * 512, n)
def pack4(w):
    words, scales = pack_weight(w, "e2m1")
    return words.reshape(words.shape[0], 128, -1), scales


def unpack4(words, scales):
    return unpack_weight(words.reshape(words.shape[0], 128, -1, 2), scales, "e2m1")


T, D, B, V = 512, 2048, 1024, 4096


def setup_inputs():
    s = mx_kscale(D)
    t = mx_kscale(B)
    hidden = np.random.standard_normal((D, T)) * s[:, None]
    proj = 2.0 * np.random.standard_normal((D, B)) / np.sqrt(D) / s[:, None]
    code = np.random.standard_normal((B, V)) / np.sqrt(B) / t[:, None]
    trust = (1.0 + 0.1 * np.random.standard_normal(B)) * t
    prior = 0.5 * np.random.standard_normal(V)
    hid_words, hid_scales = pack4(hidden)
    proj_words, proj_scales = pack4(proj)
    code_words, code_scales = pack_weight(code, "e4m3")
    return {"hid_words": hid_words, "hid_scales": hid_scales,
            "proj_words": proj_words, "proj_scales": proj_scales,
            "code_words": code_words, "code_scales": code_scales,
            "trust": bf(trust), "prior": bf(prior)}


def reference(hid_words, hid_scales, proj_words, proj_scales, code_words, code_scales, trust, prior):
    hidden = unpack4(hid_words, hid_scales)
    proj = unpack4(proj_words, proj_scales)
    code = unpack_weight(code_words, code_scales, "e4m3")
    z = hidden.T @ proj
    cost = np.log(1.0 + np.exp(-z)) * f64(trust)
    scores = mxq(cost, 1, "e4m3") @ code
    return f64(prior) - scores

@@ -1,0 +1,384 @@
+from contextlib import ExitStack
+
+import concourse.mybir as mybir
+from concourse.masks import make_identity
+
+T, D, B, V = 512, 2048, 1024, 4096
+FLOPS = 2 * T * D * B + 2 * T * B * V
+
+F32 = mybir.dt.float32
+BF16 = mybir.dt.bfloat16
+I32 = mybir.dt.int32
+U32 = mybir.dt.uint32
+U8 = mybir.dt.uint8
+E4M3X4 = mybir.dt.float8_e4m3fn_x4
+E2M1X4 = mybir.dt.float4_e2m1fn_x4
+ALU = mybir.AluOpType
+ACT = mybir.ActivationFunctionType
+
+P = 128
+K_PASS = 512
+KG1 = D // K_PASS
+KG2 = B // K_PASS
+TILES = T // P
+NV = 512
+VC = V // NV
+EPS = 2.0**-60
+WARM = 0
+PC = 2
+PLAN = [
+    ("sig", 0, 0),
+    ("sig", 0, 1),
+    ("sig", 1, 0),
+    ("s1", 2, 0),
+    ("sig", 1, 1),
+    ("log", 0, 0),
+    ("s1", 2, 1),
+    ("s1", 3, 0),
+    ("soft", 0, 0),
+    ("log", 0, 1),
+    ("s1", 3, 1),
+    ("log", 1, 0),
+    ("weigh", 0, 0, "v"),
+    ("log", 1, 1),
+    ("soft", 0, 1),
+    ("turn", 0, 0),
+    ("sig", 2, 0),
+    ("weigh", 0, 1, "v"),
+    ("group", 0, 0, "v"),
+    ("turn", 0, 1),
+    ("zc", 3, 0),
+    ("quant", 0, 0),
+    ("group", 0, 1, "v"),
+    ("sig", 2, 1),
+    ("soft", 1, 0),
+    ("sig", 3, 0),
+    ("quant", 0, 1),
+    ("weigh", 1, 0, "g"),
+    ("soft", 1, 1),
+    ("sig", 3, 1),
+    ("score", 0, 0),
+    ("zc", 3, 1),
+    ("log", 2, 0),
+    ("score", 0, 1),
+    ("weigh", 1, 1, "g"),
+    ("evV", 0),
+    ("turn", 1, 0),
+    ("score", 0, 2),
+    ("evV", 1),
+    ("score", 0, 3),
+    ("evV", 2),
+    ("turn", 1, 1),
+    ("group", 1, 0, "s"),
+    ("score", 0, 4),
+    ("log", 2, 1),
+    ("evV", 3),
+    ("score", 0, 5),
+    ("group", 1, 1, "s"),
+    ("quant", 1, 0),
+    ("soft", 2, 0),
+    ("evS", 4),
+    ("score", 0, 6),
+    ("quant", 1, 1),
+    ("evS", 5),
+    ("score", 0, 7),
+    ("weigh", 2, 0, "g"),
+    ("soft", 2, 1),
+    ("log", 3, 0),
+    ("score", 1, 0),
+    ("evV", 6),
+    ("log", 3, 1),
+    ("score", 1, 1),
+    ("add", 4),
+    ("evV", 7),
+    ("evS", 8),
+    ("turn", 2, 0),
+    ("score", 1, 2),
+    ("evV", 9),
+    ("add", 5),
+    ("group", 2, 0, "s"),
+    ("score", 1, 3),
+    ("evV", 10),
+    ("score", 1, 4),
+    ("weigh", 2, 1, "g"),
+    ("evV", 11),
+    ("score", 1, 5),
+    ("evV", 12),
+    ("score", 1, 6),
+    ("add", 8),
+    ("evS", 13),
+    ("turn", 2, 1),
+    ("score", 1, 7),
+    ("evV", 14),
+    ("group", 2, 1, "s"),
+    ("add", 13),
+    ("evV", 15),
+    ("quant", 2, 0),
+    ("quant", 2, 1),
+    ("soft", 3, 0),
+    ("score", 2, 0),
+    ("soft", 3, 1),
+    ("weigh", 3, 0, "g"),
+    ("score", 2, 1),
+    ("evV", 16),
+    ("score", 2, 2),
+    ("evV", 17),
+    ("score", 2, 3),
+    ("weigh", 3, 1, "v"),
+    ("evS", 18),
+    ("turn", 3, 0),
+    ("score", 2, 4),
+    ("evV", 19),
+    ("group", 3, 0, "s"),
+    ("add", 18),
+    ("turn", 3, 1),
+    ("score", 2, 5),
+    ("evV", 20),
+    ("group", 3, 1, "s"),
+    ("score", 2, 6),
+    ("quant", 3, 0),
+    ("evV", 21),
+    ("score", 2, 7),
+    ("quant", 3, 1),
+    ("evS", 22),
+    ("score", 3, 0),
+    ("evV", 23),
+    ("add", 22),
+    ("score", 3, 1),
+    ("evV", 24),
+    ("score", 3, 2),
+    ("evV", 25),
+    ("score", 3, 3),
+    ("evV", 26),
+    ("score", 3, 4),
+    ("evS", 27),
+    ("score", 3, 5),
+    ("evV", 28),
+    ("score", 3, 6),
+    ("add", 27),
+    ("evV", 29),
+    ("score", 3, 7),
+    ("evV", 30),
+    ("evV", 31),
+]
+
+
+def tile_vocabulary_code_scores_s4_kernel(
+    tc, hid_words, hid_scales, proj_words, proj_scales, code_words, code_scales, trust, prior, out
+):
+    nc = tc.nc
+    with ExitStack() as ctx:
+        keep = ctx.enter_context(tc.tile_pool(name="keep", bufs=1))
+        work = ctx.enter_context(tc.tile_pool(name="work", bufs=4))
+        outs = ctx.enter_context(tc.tile_pool(name="outs", bufs=6))
+        psum = ctx.enter_context(tc.psum_pool(name="psum", bufs=8))
+        ctx.enter_context(tc.manual_schedule())
+
+        h_sc = keep.tile([P, KG1, T], U8, name="h_sc", align_bytes=64)
+        e_sc = keep.tile([P, KG1, B], U8, name="e_sc", align_bytes=64)
+        c_sc = keep.tile([P, V], U8, name="c_sc", align_bytes=64)
+        ident = keep.tile([P, P], F32, name="ident", align_bytes=64)
+        warm = keep.tile([P, 1], F32, name="warm")
+        trust_b = keep.tile([P, B], BF16, name="trust_b", align_bytes=64)
+        prior_b = keep.tile([P, V], BF16, name="prior_b", align_bytes=64)
+
+        nc.vector.memset(e_sc[:].rearrange("p g n -> p (g n)").bitcast(I32), 0)
+        nc.vector.memset(h_sc[:].rearrange("p g n -> p (g n)").bitcast(I32), 0)
+        nc.vector.memset(warm[:], 0.0)
+
+
+        def load_e_scales(q):
+            nc.sync.dma_start(
+                out=e_sc[32 * q : 32 * q + 4, :, :].bitcast(I32),
+                in_=proj_scales[:, 4 * q : 4 * q + 4, :].rearrange("g r n -> r g n").bitcast(I32),
+            )
+
+        def load_h_scales(q):
+            nc.sync.dma_start(
+                out=h_sc[32 * q : 32 * q + 4, :, :].bitcast(I32),
+                in_=hid_scales[:, 4 * q : 4 * q + 4, :].rearrange("g r n -> r g n").bitcast(I32),
+            )
+
+        h_w = keep.tile([P, KG1, 2 * T], U8, name="h_w", align_bytes=64)
+        e_w = [keep.tile([P, 2, 2 * B], U8, name=f"e_w{j}", align_bytes=64) for j in range(2)]
+        def load_e_words(j):
+            nc.gpsimd.dma_start(
+                out=e_w[j][:].bitcast(I32),
+                in_=proj_words[2 * j : 2 * j + 2].rearrange("g p n -> p g n").bitcast(I32),
+            )
+
+        load_e_words(0)
+        load_e_words(1)
+        make_identity(nc, ident[:])
+        nc.gpsimd.memset(c_sc[:].bitcast(I32), 0)
+        nc.sync.dma_start(out=h_w[:].bitcast(I32), in_=hid_words.rearrange("g p n -> p g n").bitcast(I32))
+        for q in range(4):
+            load_e_scales(q)
+        for q in range(4):
+            load_h_scales(q)
+        nc.scalar.activation(out=warm[:], in_=warm[:], func=ACT.Sigmoid)
+        c_w = []
+        for v in range(VC // 2):
+            c = keep.tile([P, KG2, 2 * NV], U32, name=f"c{v}", align_bytes=64)
+            nc.sync.dma_start(
+                out=c[:].bitcast(I32),
+                in_=code_words[:, :, 2 * NV * v : 2 * NV * (v + 1), :].rearrange("g p n t -> p g (n t)").bitcast(I32),
+            )
+            c_w.append(c)
+            if v == 1:
+                nc.sync.dma_start(out=prior_b[:], in_=prior.partition_broadcast(P))
+            if v == 0:
+                nc.sync.dma_start(out=trust_b[:], in_=trust.partition_broadcast(P))
+                for q in range(4):
+                    nc.sync.dma_start(
+                        out=c_sc[32 * q : 32 * q + 8, :].bitcast(I32),
+                        in_=code_scales[:, 4 * q : 4 * q + 4, :].bitcast(I32),
+                    )
+
+        z, s, ln, y, a, xt, grp, codes, scal, zc = {}, {}, {}, {}, {}, {}, {}, {}, {}, {}
+
+        def first_product(i, g, k):
+            if k == 0:
+                z[i, g] = psum.tile([P, K_PASS], F32, name="z", tag="bank")
+            nc.tensor.matmul_mx(
+                out=z[i, g][:],
+                lhsT=h_w[:, k, 256 * i : 256 * (i + 1)].bitcast(E2M1X4),
+                lhsT_scale=h_sc[:, k, P * i : P * (i + 1)],
+                rhs=e_w[k // 2][:, k % 2, 1024 * g : 1024 * (g + 1)].bitcast(E2M1X4),
+                rhs_scale=e_sc[:, k, K_PASS * g : K_PASS * (g + 1)],
+                start=(k == 0),
+                stop=(k == KG1 - 1),
+            )
+
+        def copy_z(i, g):
+            zc[i, g] = work.tile([P, K_PASS], F32, name="zc", tag="zc")
+            nc.vector.tensor_copy(out=zc[i, g][:], in_=z[i, g][:])
+
+        def sigmoid(i, g, src):
+            s[i, g] = work.tile([P, K_PASS], F32, name="s", tag="s")
+            nc.scalar.activation(out=s[i, g][:], in_=src[:], func=ACT.Sigmoid)
+
+        def log(i, g, pieces=1):
+            ln[i, g] = work.tile([P, K_PASS], F32, name="ln", tag="ln")
+            for c in cuts(pieces):
+                nc.scalar.activation(out=ln[i, g][:, c], in_=s[i, g][:, c], func=ACT.Ln, bias=EPS)
+
+        def cuts(pieces):
+            w = K_PASS // pieces
+            return [slice(w * c, w * (c + 1)) for c in range(pieces)]
+
+        def soft(i, g, src, pieces=1):
+            y[i, g] = work.tile([P, K_PASS], F32, name="y", tag="y")
+            for c in cuts(pieces):
+                nc.vector.tensor_tensor(out=y[i, g][:, c], in0=src[:, c], in1=ln[i, g][:, c], op=ALU.min)
+
+        def weigh(engine, i, g, pieces=1):
+            a[i, g] = work.tile([P, K_PASS], BF16, name="a", tag="a", align_bytes=64)
+            nt = trust_b[:, K_PASS * g : K_PASS * (g + 1)]
+            for c in cuts(pieces):
+                engine.tensor_tensor(out=a[i, g][:, c], in0=y[i, g][:, c], in1=nt[:, c], op=ALU.mult)
+
+        def turn(i, g):
+            words = a[i, g][:].bitcast(F32)
+            xt[i, g] = psum.tile([P, 2, P], F32, name="xt", tag="bank")
+            for u in range(2):
+                nc.tensor.transpose(xt[i, g][:, u, :], words[:, u:256:2], ident[:])
+
+        def group(i, g, scalar=False):
+            grp[i, g] = work.tile([P, P, 4], BF16, name="grp", tag="grp", align_bytes=64)
+            dst = grp[i, g][:].rearrange("p r k -> p (r k)").bitcast(F32).rearrange("p (r u) -> p r u", u=2)
+            src = xt[i, g][:].rearrange("p u r -> p r u")
+            if scalar:
+                nc.scalar.copy(out=dst, in_=src)
+            else:
+                nc.vector.tensor_copy(out=dst, in_=src)
+
+        def quantise(i, g):
+            codes[i, g] = keep.tile([P, P], U32, name=f"codes{i}{g}", align_bytes=64)
+            scal[i, g] = keep.tile([P, P], U8, name=f"scal{i}{g}", align_bytes=64)
+            nc.vector.quantize_mx(
+                out=codes[i, g][:].bitcast(E4M3X4),
+                scales=scal[i, g][:],
+                in_=grp[i, g][:].rearrange("p r k -> p (r k)"),
+            )
+
+        o, acc, raw, seen = {}, {}, {}, {}
+
+        def multiply(i, v):
+            acc[i, v] = psum.tile([P, NV], F32, name="acc", tag="bank")
+            half = v % 2
+            for g in range(KG2):
+                nc.tensor.matmul_mx(
+                    out=acc[i, v][:],
+                    lhsT=codes[i, g][:].bitcast(E4M3X4),
+                    lhsT_scale=scal[i, g][:],
+                    rhs=c_w[v // 2][:, g, NV * half : NV * (half + 1)].bitcast(E4M3X4),
+                    rhs_scale=c_sc[4 * g :, NV * v : NV * (v + 1)],
+                    start=(g == 0),
+                    stop=(g == KG2 - 1),
+                )
+
+        def leave_raw(i, v):
+            raw[i, v] = work.tile([P, NV], F32, name="raw", tag="raw")
+            nc.scalar.copy(out=raw[i, v][:], in_=acc[i, v][:])
+
+        def leave(i, v, through):
+            pair = (i, v // 2)
+            if pair not in o:
+                o[pair] = outs.tile([P, 2 * NV], F32, name="o", tag="o")
+                seen[pair] = 0
+            half = v % 2
+            dst = o[pair][:, NV * half : NV * (half + 1)]
+            pri = prior_b[:, NV * v : NV * (v + 1)]
+            if through:
+                nc.gpsimd.tensor_tensor(out=dst, in0=pri, in1=raw[i, v][:], op=ALU.add)
+            else:
+                nc.vector.tensor_tensor(out=dst, in0=pri, in1=acc[i, v][:], op=ALU.add)
+            seen[pair] += 1
+            rows_i = slice(P * i, P * (i + 1))
+            if pair == (TILES - 1, VC // 2 - 1):
+                nc.sync.dma_start(out=out[rows_i, NV * v : NV * (v + 1)], in_=dst)
+            elif seen[pair] == 2:
+                w0 = 2 * NV * (v // 2)
+                nc.sync.dma_start(out=out[rows_i, w0 : w0 + 2 * NV], in_=o[pair][:])
+
+        for g in range(KG2):
+            for k in range(KG1):
+                first_product(0, g, k)
+        for g in range(KG2):
+            for k in range(KG1):
+                first_product(1, g, k)
+        eng = {"v": nc.vector, "g": nc.gpsimd}
+        def run_item(it):
+            kind = it[0]
+            if kind == "s1":
+                for k in range(KG1):
+                    first_product(it[1], it[2], k)
+            if kind == "zc":
+                copy_z(it[1], it[2])
+            if kind == "soft":
+                i, g = it[1], it[2]
+                soft(i, g, zc[i, g] if (i, g) in zc else z[i, g], PC if i == 0 else 1)
+            if kind == "weigh":
+                weigh(eng[it[3]], it[1], it[2], PC if it[1] == 0 else 1)
+            if kind == "sig":
+                i, g = it[1], it[2]
+                sigmoid(i, g, zc[i, g] if (i, g) in zc else z[i, g])
+            if kind == "log":
+                log(it[1], it[2], PC if it[1] == 0 else 1)
+            if kind == "turn":
+                turn(it[1], it[2])
+            if kind == "group":
+                group(it[1], it[2], it[3] == "s")
+            if kind == "quant":
+                quantise(it[1], it[2])
+            if kind == "score":
+                multiply(it[1], it[2])
+            if kind == "evV":
+                leave(it[1] // 8, it[1] % 8, False)
+            if kind == "evS":
+                leave_raw(it[1] // 8, it[1] % 8)
+            if kind == "add":
+                leave(it[1] // 8, it[1] % 8, True)
+        for it in PLAN:
+            run_item(it)

@@ -27,138 +27,134 @@ EPS = 2.0**-60
 WARM = 0
 PC = 2
 PLAN = [
-    ("sig", 0, 0),
-    ("sig", 0, 1),
-    ("sig", 1, 0),
     ("s1", 2, 0),
+    ("s1", 2, 1),
+    ("sig", 0, 1),
+    ("s1", 3, 1),
+    ("sig", 0, 0),
+    ("sig", 1, 0),
     ("sig", 1, 1),
     ("log", 0, 0),
-    ("s1", 2, 1),
+    ("log", 0, 1),
     ("s1", 3, 0),
     ("soft", 0, 0),
-    ("log", 0, 1),
-    ("s1", 3, 1),
-    ("log", 1, 0),
-    ("weigh", 0, 0, "v"),
-    ("log", 1, 1),
     ("soft", 0, 1),
+    ("weigh", 0, 0, "g"),
     ("turn", 0, 0),
-    ("sig", 2, 0),
-    ("weigh", 0, 1, "v"),
-    ("group", 0, 0, "v"),
-    ("turn", 0, 1),
-    ("zc", 3, 0),
-    ("quant", 0, 0),
-    ("group", 0, 1, "v"),
-    ("sig", 2, 1),
+    ("log", 1, 0),
+    ("log", 1, 1),
+    ("weigh", 0, 1, "g"),
     ("soft", 1, 0),
-    ("sig", 3, 0),
-    ("quant", 0, 1),
-    ("weigh", 1, 0, "g"),
+    ("sig", 2, 0),
     ("soft", 1, 1),
+    ("turn", 0, 1),
+    ("sig", 2, 1),
+    ("sig", 3, 0),
     ("sig", 3, 1),
-    ("score", 0, 0),
-    ("zc", 3, 1),
-    ("log", 2, 0),
-    ("score", 0, 1),
-    ("weigh", 1, 1, "g"),
-    ("evV", 0),
-    ("turn", 1, 0),
-    ("score", 0, 2),
-    ("evV", 1),
-    ("score", 0, 3),
-    ("evV", 2),
-    ("turn", 1, 1),
-    ("group", 1, 0, "s"),
-    ("score", 0, 4),
+    ("group", 0, 0, "v"),
     ("log", 2, 1),
-    ("evV", 3),
-    ("score", 0, 5),
-    ("group", 1, 1, "s"),
-    ("quant", 1, 0),
-    ("soft", 2, 0),
-    ("evS", 4),
-    ("score", 0, 6),
-    ("quant", 1, 1),
-    ("evS", 5),
-    ("score", 0, 7),
-    ("weigh", 2, 0, "g"),
-    ("soft", 2, 1),
-    ("log", 3, 0),
-    ("score", 1, 0),
-    ("evV", 6),
+    ("weigh", 1, 1, "v"),
+    ("weigh", 1, 0, "g"),
+    ("group", 0, 1, "v"),
+    ("log", 2, 0),
+    ("turn", 1, 1),
+    ("turn", 1, 0),
+    ("quant", 0, 0),
+    ("quant", 0, 1),
+    ("group", 1, 0, "v"),
     ("log", 3, 1),
-    ("score", 1, 1),
-    ("add", 4),
-    ("evV", 7),
-    ("evS", 8),
-    ("turn", 2, 0),
-    ("score", 1, 2),
-    ("evV", 9),
-    ("add", 5),
-    ("group", 2, 0, "s"),
-    ("score", 1, 3),
-    ("evV", 10),
-    ("score", 1, 4),
+    ("log", 3, 0),
+    ("group", 1, 1, "v"),
+    ("score", 0, 0),
+    ("evV", 0),
+    ("score", 0, 1),
+    ("evV", 1),
+    ("score", 0, 2),
+    ("evV", 2),
+    ("score", 0, 3),
+    ("evV", 3),
+    ("quant", 1, 0),
+    ("score", 0, 4),
+    ("soft", 2, 1),
+    ("evV", 4),
+    ("score", 0, 5),
+    ("evV", 5),
     ("weigh", 2, 1, "g"),
+    ("score", 0, 6),
+    ("evS", 6),
+    ("score", 0, 7),
+    ("soft", 2, 0),
+    ("evV", 7),
+    ("score", 1, 0),
+    ("weigh", 2, 0, "v"),
+    ("evV", 8),
+    ("score", 1, 1),
+    ("add", 6),
+    ("evS", 9),
+    ("score", 1, 2),
+    ("evS", 10),
+    ("score", 1, 3),
     ("evV", 11),
-    ("score", 1, 5),
-    ("evV", 12),
-    ("score", 1, 6),
-    ("add", 8),
-    ("evS", 13),
     ("turn", 2, 1),
-    ("score", 1, 7),
-    ("evV", 14),
-    ("group", 2, 1, "s"),
-    ("add", 13),
-    ("evV", 15),
-    ("quant", 2, 0),
-    ("quant", 2, 1),
-    ("soft", 3, 0),
-    ("score", 2, 0),
+    ("score", 1, 4),
     ("soft", 3, 1),
-    ("weigh", 3, 0, "g"),
-    ("score", 2, 1),
-    ("evV", 16),
-    ("score", 2, 2),
-    ("evV", 17),
-    ("score", 2, 3),
+    ("add", 9),
+    ("turn", 2, 0),
+    ("group", 2, 1, "s"),
+    ("evS", 12),
+    ("group", 2, 0, "s"),
+    ("quant", 2, 0),
+    ("score", 1, 5),
+    ("add", 10),
+    ("evV", 13),
     ("weigh", 3, 1, "v"),
-    ("evS", 18),
-    ("turn", 3, 0),
-    ("score", 2, 4),
-    ("evV", 19),
-    ("group", 3, 0, "s"),
-    ("add", 18),
+    ("soft", 3, 0),
+    ("score", 1, 6),
+    ("evS", 14),
+    ("score", 1, 7),
+    ("add", 12),
+    ("evV", 15),
+    ("score", 2, 0),
+    ("evS", 16),
+    ("score", 2, 1),
+    ("add", 14),
+    ("weigh", 3, 0, "v"),
+    ("evV", 17),
     ("turn", 3, 1),
+    ("score", 2, 2),
+    ("evS", 18),
+    ("score", 2, 3),
+    ("add", 16),
+    ("evV", 19),
+    ("score", 2, 4),
+    ("turn", 3, 0),
+    ("evS", 20),
     ("score", 2, 5),
-    ("evV", 20),
-    ("group", 3, 1, "s"),
+    ("add", 18),
+    ("group", 3, 1, "v"),
+    ("evV", 21),
+    ("group", 3, 0, "s"),
     ("score", 2, 6),
     ("quant", 3, 0),
-    ("evV", 21),
+    ("evV", 22),
     ("score", 2, 7),
-    ("quant", 3, 1),
-    ("evS", 22),
-    ("score", 3, 0),
+    ("add", 20),
     ("evV", 23),
-    ("add", 22),
-    ("score", 3, 1),
+    ("score", 3, 0),
     ("evV", 24),
-    ("score", 3, 2),
+    ("score", 3, 1),
     ("evV", 25),
-    ("score", 3, 3),
+    ("score", 3, 2),
     ("evV", 26),
+    ("score", 3, 3),
+    ("evV", 27),
     ("score", 3, 4),
-    ("evS", 27),
-    ("score", 3, 5),
     ("evV", 28),
-    ("score", 3, 6),
-    ("add", 27),
+    ("score", 3, 5),
     ("evV", 29),
-    ("score", 3, 7),
+    ("score", 3, 6),
     ("evV", 30),
+    ("score", 3, 7),
     ("evV", 31),
 ]
 
@@ -199,8 +195,15 @@ def tile_vocabulary_code_scores_s4_kernel(
                 in_=hid_scales[:, 4 * q : 4 * q + 4, :].rearrange("g r n -> r g n").bitcast(I32),
             )
 
-        h_w = keep.tile([P, KG1, 2 * T], U8, name="h_w", align_bytes=64)
+        h_w = [keep.tile([P, KG1, T], U8, name=f"h_w{j}", align_bytes=64) for j in range(2)]
         e_w = [keep.tile([P, 2, 2 * B], U8, name=f"e_w{j}", align_bytes=64) for j in range(2)]
+
+        def load_h_words(j):
+            nc.sync.dma_start(
+                out=h_w[j][:].bitcast(I32),
+                in_=hid_words[:, :, T * j : T * (j + 1)].rearrange("g p n -> p g n").bitcast(I32),
+            )
+
         def load_e_words(j):
             nc.gpsimd.dma_start(
                 out=e_w[j][:].bitcast(I32),
@@ -211,11 +214,12 @@ def tile_vocabulary_code_scores_s4_kernel(
         load_e_words(1)
         make_identity(nc, ident[:])
         nc.gpsimd.memset(c_sc[:].bitcast(I32), 0)
-        nc.sync.dma_start(out=h_w[:].bitcast(I32), in_=hid_words.rearrange("g p n -> p g n").bitcast(I32))
+        load_h_words(0)
         for q in range(4):
             load_e_scales(q)
         for q in range(4):
             load_h_scales(q)
+        load_h_words(1)
         nc.scalar.activation(out=warm[:], in_=warm[:], func=ACT.Sigmoid)
         c_w = []
         for v in range(VC // 2):
@@ -242,7 +246,7 @@ def tile_vocabulary_code_scores_s4_kernel(
                 z[i, g] = psum.tile([P, K_PASS], F32, name="z", tag="bank")
             nc.tensor.matmul_mx(
                 out=z[i, g][:],
-                lhsT=h_w[:, k, 256 * i : 256 * (i + 1)].bitcast(E2M1X4),
+                lhsT=h_w[i // 2][:, k, 256 * (i % 2) : 256 * (i % 2 + 1)].bitcast(E2M1X4),
                 lhsT_scale=h_sc[:, k, P * i : P * (i + 1)],
                 rhs=e_w[k // 2][:, k % 2, 1024 * g : 1024 * (g + 1)].bitcast(E2M1X4),
                 rhs_scale=e_sc[:, k, K_PASS * g : K_PASS * (g + 1)],
@@ -285,21 +289,22 @@ def tile_vocabulary_code_scores_s4_kernel(
                 nc.tensor.transpose(xt[i, g][:, u, :], words[:, u:256:2], ident[:])
 
         def group(i, g, scalar=False):
-            grp[i, g] = work.tile([P, P, 4], BF16, name="grp", tag="grp", align_bytes=64)
-            dst = grp[i, g][:].rearrange("p r k -> p (r k)").bitcast(F32).rearrange("p (r u) -> p r u", u=2)
+            if i not in grp:
+                grp[i] = work.tile([P, KG2, 4 * P], BF16, name="grp", tag="grp", align_bytes=64)
+                codes[i] = keep.tile([P, KG2, P], U32, name=f"codes{i}", align_bytes=64)
+                scal[i] = keep.tile([P, KG2, P], U8, name=f"scal{i}", align_bytes=64)
+            dst = grp[i][:, g, :].bitcast(F32).rearrange("p (r u) -> p r u", u=2)
             src = xt[i, g][:].rearrange("p u r -> p r u")
             if scalar:
                 nc.scalar.copy(out=dst, in_=src)
             else:
                 nc.vector.tensor_copy(out=dst, in_=src)
 
-        def quantise(i, g):
-            codes[i, g] = keep.tile([P, P], U32, name=f"codes{i}{g}", align_bytes=64)
-            scal[i, g] = keep.tile([P, P], U8, name=f"scal{i}{g}", align_bytes=64)
+        def quantise(i, g0, g1):
             nc.vector.quantize_mx(
-                out=codes[i, g][:].bitcast(E4M3X4),
-                scales=scal[i, g][:],
-                in_=grp[i, g][:].rearrange("p r k -> p (r k)"),
+                out=codes[i][:, g0:g1, :].rearrange("p g r -> p (g r)").bitcast(E4M3X4),
+                scales=scal[i][:, g0:g1, :].rearrange("p g r -> p (g r)"),
+                in_=grp[i][:, g0:g1, :].rearrange("p g r -> p (g r)"),
             )
 
         o, acc, raw, seen = {}, {}, {}, {}
@@ -310,8 +315,8 @@ def tile_vocabulary_code_scores_s4_kernel(
             for g in range(KG2):
                 nc.tensor.matmul_mx(
                     out=acc[i, v][:],
-                    lhsT=codes[i, g][:].bitcast(E4M3X4),
-                    lhsT_scale=scal[i, g][:],
+                    lhsT=codes[i][:, g, :].bitcast(E4M3X4),
+                    lhsT_scale=scal[i][:, g, :],
                     rhs=c_w[v // 2][:, g, NV * half : NV * (half + 1)].bitcast(E4M3X4),
                     rhs_scale=c_sc[4 * g :, NV * v : NV * (v + 1)],
                     start=(g == 0),
@@ -336,7 +341,7 @@ def tile_vocabulary_code_scores_s4_kernel(
                 nc.vector.tensor_tensor(out=dst, in0=pri, in1=acc[i, v][:], op=ALU.add)
             seen[pair] += 1
             rows_i = slice(P * i, P * (i + 1))
-            if pair == (TILES - 1, VC // 2 - 1):
+            if pair in ((0, 0), (TILES - 1, VC // 2 - 1)):
                 nc.sync.dma_start(out=out[rows_i, NV * v : NV * (v + 1)], in_=dst)
             elif seen[pair] == 2:
                 w0 = 2 * NV * (v // 2)
@@ -371,7 +376,7 @@ def tile_vocabulary_code_scores_s4_kernel(
             if kind == "group":
                 group(it[1], it[2], it[3] == "s")
             if kind == "quant":
-                quantise(it[1], it[2])
+                quantise(it[1], it[2] if it[1] == 0 else 0, it[2] + 1 if it[1] == 0 else 2)
             if kind == "score":
                 multiply(it[1], it[2])
             if kind == "evV":

@@ -27,118 +27,115 @@ EPS = 2.0**-60
 WARM = 0
 PC = 2
 PLAN = [
-    ("s1", 2, 0),
-    ("s1", 2, 1),
-    ("sig", 0, 1),
     ("s1", 3, 1),
     ("sig", 0, 0),
+    ("sig", 0, 1),
     ("sig", 1, 0),
     ("sig", 1, 1),
+    ("s1", 3, 0),
     ("log", 0, 0),
     ("log", 0, 1),
-    ("s1", 3, 0),
-    ("soft", 0, 0),
-    ("soft", 0, 1),
-    ("weigh", 0, 0, "g"),
-    ("turn", 0, 0),
-    ("log", 1, 0),
+    ("s1", 2, 1),
     ("log", 1, 1),
-    ("weigh", 0, 1, "g"),
-    ("soft", 1, 0),
-    ("sig", 2, 0),
-    ("soft", 1, 1),
-    ("turn", 0, 1),
+    ("soft", 0, 0),
+    ("log", 1, 0),
+    ("s1", 2, 0),
+    ("soft", 0, 1),
     ("sig", 2, 1),
+    ("weigh", 0, 0, "v"),
+    ("soft", 1, 0),
+    ("soft", 1, 1),
+    ("weigh", 0, 1, "g"),
+    ("sig", 2, 0),
     ("sig", 3, 0),
-    ("sig", 3, 1),
+    ("turn", 0, 0),
+    ("turn", 0, 1),
     ("group", 0, 0, "v"),
-    ("log", 2, 1),
+    ("sig", 3, 1),
     ("weigh", 1, 1, "v"),
-    ("weigh", 1, 0, "g"),
     ("group", 0, 1, "v"),
-    ("log", 2, 0),
-    ("turn", 1, 1),
-    ("turn", 1, 0),
     ("quant", 0, 0),
+    ("turn", 1, 1),
+    ("log", 2, 1),
+    ("weigh", 1, 0, "g"),
+    ("log", 3, 1),
+    ("turn", 1, 0),
     ("quant", 0, 1),
     ("group", 1, 0, "v"),
-    ("log", 3, 1),
-    ("log", 3, 0),
+    ("log", 2, 0),
     ("group", 1, 1, "v"),
+    ("log", 3, 0),
     ("score", 0, 0),
     ("evV", 0),
     ("score", 0, 1),
     ("evV", 1),
     ("score", 0, 2),
+    ("quant", 1, 0),
     ("evV", 2),
     ("score", 0, 3),
-    ("evV", 3),
-    ("quant", 1, 0),
-    ("score", 0, 4),
     ("soft", 2, 1),
+    ("evV", 3),
+    ("score", 0, 4),
     ("evV", 4),
-    ("score", 0, 5),
-    ("evV", 5),
     ("weigh", 2, 1, "g"),
+    ("score", 0, 5),
+    ("soft", 2, 0),
+    ("evV", 5),
     ("score", 0, 6),
+    ("weigh", 2, 0, "v"),
     ("evS", 6),
     ("score", 0, 7),
-    ("soft", 2, 0),
     ("evV", 7),
     ("score", 1, 0),
-    ("weigh", 2, 0, "v"),
     ("evV", 8),
-    ("score", 1, 1),
     ("add", 6),
-    ("evS", 9),
+    ("score", 1, 1),
+    ("evV", 9),
     ("score", 1, 2),
     ("evS", 10),
     ("score", 1, 3),
     ("evV", 11),
-    ("turn", 2, 1),
-    ("score", 1, 4),
     ("soft", 3, 1),
-    ("add", 9),
-    ("turn", 2, 0),
-    ("group", 2, 1, "s"),
+    ("score", 1, 4),
     ("evS", 12),
+    ("turn", 2, 0),
+    ("add", 10),
+    ("turn", 2, 1),
+    ("group", 2, 1, "s"),
+    ("score", 1, 5),
     ("group", 2, 0, "s"),
     ("quant", 2, 0),
-    ("score", 1, 5),
-    ("add", 10),
     ("evV", 13),
-    ("weigh", 3, 1, "v"),
-    ("soft", 3, 0),
     ("score", 1, 6),
+    ("soft", 3, 0),
     ("evS", 14),
-    ("score", 1, 7),
     ("add", 12),
+    ("score", 1, 7),
     ("evV", 15),
+    ("weigh", 3, 1, "v"),
     ("score", 2, 0),
-    ("evS", 16),
-    ("score", 2, 1),
+    ("evV", 16),
     ("add", 14),
-    ("weigh", 3, 0, "v"),
+    ("score", 2, 1),
     ("evV", 17),
-    ("turn", 3, 1),
     ("score", 2, 2),
-    ("evS", 18),
+    ("evV", 18),
     ("score", 2, 3),
-    ("add", 16),
     ("evV", 19),
+    ("weigh", 3, 0, "g"),
     ("score", 2, 4),
-    ("turn", 3, 0),
     ("evS", 20),
     ("score", 2, 5),
-    ("add", 18),
-    ("group", 3, 1, "v"),
     ("evV", 21),
-    ("group", 3, 0, "s"),
+    ("turn", 3, 1),
+    ("group", 3, 1, "s"),
+    ("turn", 3, 0),
     ("score", 2, 6),
+    ("group", 3, 0, "s"),
     ("quant", 3, 0),
     ("evV", 22),
-    ("score", 2, 7),
     ("add", 20),
+    ("score", 2, 7),
     ("evV", 23),
     ("score", 3, 0),
     ("evV", 24),

@@ -18,142 +18,15 @@ ACT = mybir.ActivationFunctionType
 
 P = 128
 K_PASS = 512
-KG1 = D // K_PASS
-KG2 = B // K_PASS
+BANK = 512
+D_PASSES = D // K_PASS
+GROUPS = B // K_PASS
 TILES = T // P
-NV = 512
-VC = V // NV
+CHUNKS = V // BANK
 EPS = 2.0**-60
-WARM = 0
-PC = 2
-PLAN = [
-    ("s1", 3, 1),
-    ("sig", 0, 0),
-    ("sig", 0, 1),
-    ("sig", 1, 0),
-    ("sig", 1, 1),
-    ("s1", 3, 0),
-    ("log", 0, 0),
-    ("log", 0, 1),
-    ("s1", 2, 1),
-    ("log", 1, 1),
-    ("soft", 0, 0),
-    ("log", 1, 0),
-    ("s1", 2, 0),
-    ("soft", 0, 1),
-    ("sig", 2, 1),
-    ("weigh", 0, 0, "v"),
-    ("soft", 1, 0),
-    ("soft", 1, 1),
-    ("weigh", 0, 1, "g"),
-    ("sig", 2, 0),
-    ("sig", 3, 0),
-    ("turn", 0, 0),
-    ("turn", 0, 1),
-    ("group", 0, 0, "v"),
-    ("sig", 3, 1),
-    ("weigh", 1, 1, "v"),
-    ("group", 0, 1, "v"),
-    ("quant", 0, 0),
-    ("turn", 1, 1),
-    ("log", 2, 1),
-    ("weigh", 1, 0, "g"),
-    ("log", 3, 1),
-    ("turn", 1, 0),
-    ("quant", 0, 1),
-    ("group", 1, 0, "v"),
-    ("log", 2, 0),
-    ("group", 1, 1, "v"),
-    ("log", 3, 0),
-    ("score", 0, 0),
-    ("evV", 0),
-    ("score", 0, 1),
-    ("evV", 1),
-    ("score", 0, 2),
-    ("quant", 1, 0),
-    ("evV", 2),
-    ("score", 0, 3),
-    ("soft", 2, 1),
-    ("evV", 3),
-    ("score", 0, 4),
-    ("evV", 4),
-    ("weigh", 2, 1, "g"),
-    ("score", 0, 5),
-    ("soft", 2, 0),
-    ("evV", 5),
-    ("score", 0, 6),
-    ("weigh", 2, 0, "v"),
-    ("evS", 6),
-    ("score", 0, 7),
-    ("evV", 7),
-    ("score", 1, 0),
-    ("evV", 8),
-    ("add", 6),
-    ("score", 1, 1),
-    ("evV", 9),
-    ("score", 1, 2),
-    ("evS", 10),
-    ("score", 1, 3),
-    ("evV", 11),
-    ("soft", 3, 1),
-    ("score", 1, 4),
-    ("evS", 12),
-    ("turn", 2, 0),
-    ("add", 10),
-    ("turn", 2, 1),
-    ("group", 2, 1, "s"),
-    ("score", 1, 5),
-    ("group", 2, 0, "s"),
-    ("quant", 2, 0),
-    ("evV", 13),
-    ("score", 1, 6),
-    ("soft", 3, 0),
-    ("evS", 14),
-    ("add", 12),
-    ("score", 1, 7),
-    ("evV", 15),
-    ("weigh", 3, 1, "v"),
-    ("score", 2, 0),
-    ("evV", 16),
-    ("add", 14),
-    ("score", 2, 1),
-    ("evV", 17),
-    ("score", 2, 2),
-    ("evV", 18),
-    ("score", 2, 3),
-    ("evV", 19),
-    ("weigh", 3, 0, "g"),
-    ("score", 2, 4),
-    ("evS", 20),
-    ("score", 2, 5),
-    ("evV", 21),
-    ("turn", 3, 1),
-    ("group", 3, 1, "s"),
-    ("turn", 3, 0),
-    ("score", 2, 6),
-    ("group", 3, 0, "s"),
-    ("quant", 3, 0),
-    ("evV", 22),
-    ("add", 20),
-    ("score", 2, 7),
-    ("evV", 23),
-    ("score", 3, 0),
-    ("evV", 24),
-    ("score", 3, 1),
-    ("evV", 25),
-    ("score", 3, 2),
-    ("evV", 26),
-    ("score", 3, 3),
-    ("evV", 27),
-    ("score", 3, 4),
-    ("evV", 28),
-    ("score", 3, 5),
-    ("evV", 29),
-    ("score", 3, 6),
-    ("evV", 30),
-    ("score", 3, 7),
-    ("evV", 31),
-]
+
+BY_SCALAR = (6, 9, 10, 18, 28)
+ADD_LATER = 2
 
 
 def tile_vocabulary_code_scores_s4_kernel(
@@ -167,220 +40,235 @@ def tile_vocabulary_code_scores_s4_kernel(
         psum = ctx.enter_context(tc.psum_pool(name="psum", bufs=8))
         ctx.enter_context(tc.manual_schedule())
 
-        h_sc = keep.tile([P, KG1, T], U8, name="h_sc", align_bytes=64)
-        e_sc = keep.tile([P, KG1, B], U8, name="e_sc", align_bytes=64)
-        c_sc = keep.tile([P, V], U8, name="c_sc", align_bytes=64)
-        ident = keep.tile([P, P], F32, name="ident", align_bytes=64)
+        h_scales = keep.tile([P, D_PASSES, T], U8, name="h_scales", align_bytes=64)
+        e_scales = keep.tile([P, D_PASSES, B], U8, name="e_scales", align_bytes=64)
+        c_scales = keep.tile([P, V], U8, name="c_scales", align_bytes=64)
+        rows = keep.tile([P, 32], F32, name="rows", align_bytes=64)
         warm = keep.tile([P, 1], F32, name="warm")
-        trust_b = keep.tile([P, B], BF16, name="trust_b", align_bytes=64)
-        prior_b = keep.tile([P, V], BF16, name="prior_b", align_bytes=64)
-
-        nc.vector.memset(e_sc[:].rearrange("p g n -> p (g n)").bitcast(I32), 0)
-        nc.vector.memset(h_sc[:].rearrange("p g n -> p (g n)").bitcast(I32), 0)
+        nc.vector.memset(e_scales[:].rearrange("p g n -> p (g n)").bitcast(I32), 0)
+        nc.vector.memset(h_scales[:].rearrange("p g n -> p (g n)").bitcast(I32), 0)
         nc.vector.memset(warm[:], 0.0)
+        nc.vector.memset(rows[:], 0.0)
 
-
-        def load_e_scales(q):
-            nc.sync.dma_start(
-                out=e_sc[32 * q : 32 * q + 4, :, :].bitcast(I32),
-                in_=proj_scales[:, 4 * q : 4 * q + 4, :].rearrange("g r n -> r g n").bitcast(I32),
-            )
-
-        def load_h_scales(q):
-            nc.sync.dma_start(
-                out=h_sc[32 * q : 32 * q + 4, :, :].bitcast(I32),
-                in_=hid_scales[:, 4 * q : 4 * q + 4, :].rearrange("g r n -> r g n").bitcast(I32),
-            )
-
-        h_w = [keep.tile([P, KG1, T], U8, name=f"h_w{j}", align_bytes=64) for j in range(2)]
-        e_w = [keep.tile([P, 2, 2 * B], U8, name=f"e_w{j}", align_bytes=64) for j in range(2)]
+        h_words = [keep.tile([P, D_PASSES, T], U8, name=f"h_words{j}", align_bytes=64) for j in range(2)]
+        e_words = [keep.tile([P, 2, 2 * B], U8, name=f"e_words{j}", align_bytes=64) for j in range(2)]
 
         def load_h_words(j):
             nc.sync.dma_start(
-                out=h_w[j][:].bitcast(I32),
+                out=h_words[j][:].bitcast(I32),
                 in_=hid_words[:, :, T * j : T * (j + 1)].rearrange("g p n -> p g n").bitcast(I32),
             )
 
-        def load_e_words(j):
+        for j in range(2):
             nc.gpsimd.dma_start(
-                out=e_w[j][:].bitcast(I32),
+                out=e_words[j][:].bitcast(I32),
                 in_=proj_words[2 * j : 2 * j + 2].rearrange("g p n -> p g n").bitcast(I32),
             )
-
-        load_e_words(0)
-        load_e_words(1)
+        ident = keep.tile([P, P], F32, name="ident", align_bytes=64)
         make_identity(nc, ident[:])
-        nc.gpsimd.memset(c_sc[:].bitcast(I32), 0)
+        nc.gpsimd.memset(c_scales[:].bitcast(I32), 0)
         load_h_words(0)
-        for q in range(4):
-            load_e_scales(q)
-        for q in range(4):
-            load_h_scales(q)
+        for plane, source in ((e_scales, proj_scales), (h_scales, hid_scales)):
+            for q in range(4):
+                nc.sync.dma_start(
+                    out=plane[32 * q : 32 * q + 4, :, :].bitcast(I32),
+                    in_=source[:, 4 * q : 4 * q + 4, :].rearrange("g r n -> r g n").bitcast(I32),
+                )
         load_h_words(1)
-        nc.scalar.activation(out=warm[:], in_=warm[:], func=ACT.Sigmoid)
-        c_w = []
-        for v in range(VC // 2):
-            c = keep.tile([P, KG2, 2 * NV], U32, name=f"c{v}", align_bytes=64)
+        nc.sync.dma_start(out=rows[0:64, :], in_=prior.rearrange("(c k) -> c k", k=64).bitcast(F32))
+        nc.sync.dma_start(out=rows[64:80, :], in_=trust.rearrange("(c k) -> c k", k=64).bitcast(F32))
+        c_words = []
+        for j in range(CHUNKS // 2):
+            words = keep.tile([P, GROUPS, 2 * BANK], U32, name=f"c_words{j}", align_bytes=64)
             nc.sync.dma_start(
-                out=c[:].bitcast(I32),
-                in_=code_words[:, :, 2 * NV * v : 2 * NV * (v + 1), :].rearrange("g p n t -> p g (n t)").bitcast(I32),
+                out=words[:].bitcast(I32),
+                in_=code_words[:, :, 2 * BANK * j : 2 * BANK * (j + 1), :]
+                .rearrange("g p n t -> p g (n t)")
+                .bitcast(I32),
             )
-            c_w.append(c)
-            if v == 1:
-                nc.sync.dma_start(out=prior_b[:], in_=prior.partition_broadcast(P))
-            if v == 0:
-                nc.sync.dma_start(out=trust_b[:], in_=trust.partition_broadcast(P))
+            c_words.append(words)
+            if j == 0:
                 for q in range(4):
                     nc.sync.dma_start(
-                        out=c_sc[32 * q : 32 * q + 8, :].bitcast(I32),
+                        out=c_scales[32 * q : 32 * q + 8, :].bitcast(I32),
                         in_=code_scales[:, 4 * q : 4 * q + 4, :].bitcast(I32),
                     )
+        nc.scalar.activation(out=warm[:], in_=warm[:], func=ACT.Sigmoid)
 
-        z, s, ln, y, a, xt, grp, codes, scal, zc = {}, {}, {}, {}, {}, {}, {}, {}, {}, {}
+        z, s, ln, y, a, xt, grouped, codes, scales, acc, raw, pairs = ({} for n in range(12))
 
-        def first_product(i, g, k):
-            if k == 0:
-                z[i, g] = psum.tile([P, K_PASS], F32, name="z", tag="bank")
-            nc.tensor.matmul_mx(
-                out=z[i, g][:],
-                lhsT=h_w[i // 2][:, k, 256 * (i % 2) : 256 * (i % 2 + 1)].bitcast(E2M1X4),
-                lhsT_scale=h_sc[:, k, P * i : P * (i + 1)],
-                rhs=e_w[k // 2][:, k % 2, 1024 * g : 1024 * (g + 1)].bitcast(E2M1X4),
-                rhs_scale=e_sc[:, k, K_PASS * g : K_PASS * (g + 1)],
-                start=(k == 0),
-                stop=(k == KG1 - 1),
-            )
+        def project(i, g):
+            z[i, g] = psum.tile([P, K_PASS], F32, name="z", tag="bank")
+            for k in range(D_PASSES):
+                h0, e0 = 2 * P * (i % 2), 2 * K_PASS * g
+                nc.tensor.matmul_mx(
+                    out=z[i, g][:],
+                    lhsT=h_words[i // 2][:, k, h0 : h0 + 2 * P].bitcast(E2M1X4),
+                    lhsT_scale=h_scales[:, k, P * i : P * (i + 1)],
+                    rhs=e_words[k // 2][:, k % 2, e0 : e0 + 2 * K_PASS].bitcast(E2M1X4),
+                    rhs_scale=e_scales[:, k, K_PASS * g : K_PASS * (g + 1)],
+                    start=(k == 0),
+                    stop=(k == D_PASSES - 1),
+                )
 
-        def copy_z(i, g):
-            zc[i, g] = work.tile([P, K_PASS], F32, name="zc", tag="zc")
-            nc.vector.tensor_copy(out=zc[i, g][:], in_=z[i, g][:])
-
-        def sigmoid(i, g, src):
+        def sigmoid(i, g):
             s[i, g] = work.tile([P, K_PASS], F32, name="s", tag="s")
-            nc.scalar.activation(out=s[i, g][:], in_=src[:], func=ACT.Sigmoid)
+            nc.scalar.activation(out=s[i, g][:], in_=z[i, g][:], func=ACT.Sigmoid)
 
-        def log(i, g, pieces=1):
+        def log(i, g):
             ln[i, g] = work.tile([P, K_PASS], F32, name="ln", tag="ln")
-            for c in cuts(pieces):
-                nc.scalar.activation(out=ln[i, g][:, c], in_=s[i, g][:, c], func=ACT.Ln, bias=EPS)
+            nc.scalar.activation(out=ln[i, g][:], in_=s[i, g][:], func=ACT.Ln, bias=EPS)
 
-        def cuts(pieces):
-            w = K_PASS // pieces
-            return [slice(w * c, w * (c + 1)) for c in range(pieces)]
-
-        def soft(i, g, src, pieces=1):
+        def soften(i, g):
             y[i, g] = work.tile([P, K_PASS], F32, name="y", tag="y")
-            for c in cuts(pieces):
-                nc.vector.tensor_tensor(out=y[i, g][:, c], in0=src[:, c], in1=ln[i, g][:, c], op=ALU.min)
+            nc.vector.tensor_tensor(out=y[i, g][:], in0=z[i, g][:], in1=ln[i, g][:], op=ALU.min)
 
-        def weigh(engine, i, g, pieces=1):
+        def weigh(engine, i, g):
             a[i, g] = work.tile([P, K_PASS], BF16, name="a", tag="a", align_bytes=64)
-            nt = trust_b[:, K_PASS * g : K_PASS * (g + 1)]
-            for c in cuts(pieces):
-                engine.tensor_tensor(out=a[i, g][:, c], in0=y[i, g][:, c], in1=nt[:, c], op=ALU.mult)
+            engine.tensor_tensor(
+                out=a[i, g][:], in0=y[i, g][:], in1=trust_b[:, K_PASS * g : K_PASS * (g + 1)], op=ALU.mult
+            )
 
         def turn(i, g):
             words = a[i, g][:].bitcast(F32)
             xt[i, g] = psum.tile([P, 2, P], F32, name="xt", tag="bank")
             for u in range(2):
-                nc.tensor.transpose(xt[i, g][:, u, :], words[:, u:256:2], ident[:])
+                nc.tensor.transpose(xt[i, g][:, u, :], words[:, u : K_PASS // 2 : 2], ident[:])
 
-        def group(i, g, scalar=False):
-            if i not in grp:
-                grp[i] = work.tile([P, KG2, 4 * P], BF16, name="grp", tag="grp", align_bytes=64)
-                codes[i] = keep.tile([P, KG2, P], U32, name=f"codes{i}", align_bytes=64)
-                scal[i] = keep.tile([P, KG2, P], U8, name=f"scal{i}", align_bytes=64)
-            dst = grp[i][:, g, :].bitcast(F32).rearrange("p (r u) -> p r u", u=2)
-            src = xt[i, g][:].rearrange("p u r -> p r u")
-            if scalar:
-                nc.scalar.copy(out=dst, in_=src)
-            else:
-                nc.vector.tensor_copy(out=dst, in_=src)
-
-        def quantise(i, g0, g1):
-            nc.vector.quantize_mx(
-                out=codes[i][:, g0:g1, :].rearrange("p g r -> p (g r)").bitcast(E4M3X4),
-                scales=scal[i][:, g0:g1, :].rearrange("p g r -> p (g r)"),
-                in_=grp[i][:, g0:g1, :].rearrange("p g r -> p (g r)"),
+        def group(engine_copy, i, g):
+            if i not in grouped:
+                grouped[i] = work.tile([P, GROUPS, 4 * P], BF16, name="grouped", tag="grouped", align_bytes=64)
+                codes[i] = keep.tile([P, GROUPS, P], U32, name=f"codes{i}", align_bytes=64)
+                scales[i] = keep.tile([P, GROUPS, P], U8, name=f"scales{i}", align_bytes=64)
+            engine_copy(
+                out=grouped[i][:, g, :].bitcast(F32).rearrange("p (r u) -> p r u", u=2),
+                in_=xt[i, g][:].rearrange("p u r -> p r u"),
             )
 
-        o, acc, raw, seen = {}, {}, {}, {}
+        def quantise(i, first, last):
+            nc.vector.quantize_mx(
+                out=codes[i][:, first : last + 1, :].rearrange("p g r -> p (g r)").bitcast(E4M3X4),
+                scales=scales[i][:, first : last + 1, :].rearrange("p g r -> p (g r)"),
+                in_=grouped[i][:, first : last + 1, :].rearrange("p g r -> p (g r)"),
+            )
 
-        def multiply(i, v):
-            acc[i, v] = psum.tile([P, NV], F32, name="acc", tag="bank")
-            half = v % 2
-            for g in range(KG2):
+        def score(n):
+            i, v = divmod(n, CHUNKS)
+            acc[n] = psum.tile([P, BANK], F32, name="acc", tag="bank")
+            c0 = BANK * (v % 2)
+            for g in range(GROUPS):
                 nc.tensor.matmul_mx(
-                    out=acc[i, v][:],
+                    out=acc[n][:],
                     lhsT=codes[i][:, g, :].bitcast(E4M3X4),
-                    lhsT_scale=scal[i][:, g, :],
-                    rhs=c_w[v // 2][:, g, NV * half : NV * (half + 1)].bitcast(E4M3X4),
-                    rhs_scale=c_sc[4 * g :, NV * v : NV * (v + 1)],
+                    lhsT_scale=scales[i][:, g, :],
+                    rhs=c_words[v // 2][:, g, c0 : c0 + BANK].bitcast(E4M3X4),
+                    rhs_scale=c_scales[4 * g :, BANK * v : BANK * (v + 1)],
                     start=(g == 0),
-                    stop=(g == KG2 - 1),
+                    stop=(g == GROUPS - 1),
                 )
 
-        def leave_raw(i, v):
-            raw[i, v] = work.tile([P, NV], F32, name="raw", tag="raw")
-            nc.scalar.copy(out=raw[i, v][:], in_=acc[i, v][:])
+        def finish(n, engine, sums):
+            i, v = divmod(n, CHUNKS)
+            if n // 2 not in pairs:
+                pairs[n // 2] = [outs.tile([P, 2 * BANK], F32, name="o", tag="o"), 0]
+            o = pairs[n // 2][0]
+            half = o[:, BANK * (v % 2) : BANK * (v % 2 + 1)]
+            engine.tensor_tensor(out=half, in0=prior_b[:, BANK * v : BANK * (v + 1)], in1=sums[:], op=ALU.add)
+            pairs[n // 2][1] += 1
+            tokens = slice(P * i, P * (i + 1))
+            if n // 2 in (0, TILES * CHUNKS // 2 - 1):
+                nc.sync.dma_start(out=out[tokens, BANK * v : BANK * (v + 1)], in_=half)
+            elif pairs[n // 2][1] == 2:
+                v0 = v - v % 2
+                nc.sync.dma_start(out=out[tokens, BANK * v0 : BANK * (v0 + 2)], in_=o[:])
 
-        def leave(i, v, through):
-            pair = (i, v // 2)
-            if pair not in o:
-                o[pair] = outs.tile([P, 2 * NV], F32, name="o", tag="o")
-                seen[pair] = 0
-            half = v % 2
-            dst = o[pair][:, NV * half : NV * (half + 1)]
-            pri = prior_b[:, NV * v : NV * (v + 1)]
-            if through:
-                nc.gpsimd.tensor_tensor(out=dst, in0=pri, in1=raw[i, v][:], op=ALU.add)
+        early = [(i, g) for i in (0, 1) for g in range(GROUPS)]
+        late = [(i, g) for i in (2, 3) for g in range(GROUPS)]
+
+        for g in range(GROUPS):
+            project(0, g)
+
+        rows4 = keep.tile([P, 4, 32], F32, name="rows4", align_bytes=64)
+        cols = keep.tile([P, P], F32, name="cols", align_bytes=64)
+        nc.vector.tensor_copy(out=rows4[:], in_=rows[:].unsqueeze(1).to_broadcast([P, 4, 32]))
+        turned = psum.tile([P, P], F32, name="turned", tag="bank")
+        nc.tensor.transpose(turned[:], rows4[:].rearrange("p a k -> p (a k)"), ident[:])
+        nc.vector.tensor_copy(out=cols[:], in_=turned[:])
+
+        def spread(name, first, count):
+            repeated = keep.tile([P, count, 32], F32, name=f"{name}_repeated", align_bytes=64)
+            words = keep.tile([P, 32 * count], F32, name=f"{name}_words", align_bytes=64)
+            column = cols[:, first : first + count].unsqueeze(2)
+            nc.vector.tensor_copy(out=repeated[:], in_=column.to_broadcast([P, count, 32]))
+            nc.vector.transpose(out=words[:], in_=repeated[:].rearrange("p c m -> p (c m)"))
+            return words[:].bitcast(BF16)
+
+        for g in range(GROUPS):
+            project(1, g)
+        trust_b = spread("trust", 64, 16)
+        prior_b = spread("prior", 0, 64)
+
+        for i, g in early:
+            sigmoid(i, g)
+        for i, g in late:
+            project(i, g)
+        for i, g in early:
+            log(i, g)
+        soften(0, 0)
+        soften(0, 1)
+        weigh(nc.gpsimd, 0, 0)
+        soften(1, 0)
+        soften(1, 1)
+        for i, g in late:
+            sigmoid(i, g)
+        weigh(nc.vector, 0, 1)
+        turn(0, 0)
+        turn(0, 1)
+        weigh(nc.vector, 1, 0)
+        group(nc.vector.tensor_copy, 0, 0)
+        group(nc.vector.tensor_copy, 0, 1)
+        weigh(nc.gpsimd, 1, 1)
+        quantise(0, 0, 0)
+        quantise(0, 1, 1)
+        turn(1, 0)
+        turn(1, 1)
+        group(nc.vector.tensor_copy, 1, 0)
+        group(nc.vector.tensor_copy, 1, 1)
+        for i, g in late:
+            log(i, g)
+
+        def turn_and_group(i):
+            for g in range(GROUPS):
+                turn(i, g)
+            for g in range(GROUPS):
+                group(nc.scalar.copy, i, g)
+
+        before = {
+            0: [lambda: quantise(1, 0, 1)],
+            3: [lambda: soften(2, 0)],
+            5: [lambda: soften(2, 1)],
+            10: [lambda: soften(3, 0)],
+            11: [lambda: turn_and_group(2)],
+            12: [lambda: quantise(2, 0, 1)],
+            13: [lambda: soften(3, 1)],
+            20: [lambda: turn_and_group(3)],
+            21: [lambda: quantise(3, 0, 1)],
+        }
+        after = {
+            3: [lambda: weigh(nc.gpsimd, 2, 0)],
+            5: [lambda: weigh(nc.vector, 2, 1)],
+            18: [lambda: weigh(nc.gpsimd, 3, 0), lambda: weigh(nc.gpsimd, 3, 1)],
+        }
+        for n in range(TILES * CHUNKS):
+            score(n)
+            for step in before.get(n, []):
+                step()
+            if n in BY_SCALAR:
+                raw[n] = work.tile([P, BANK], F32, name="raw", tag="raw")
+                nc.scalar.copy(out=raw[n][:], in_=acc[n][:])
             else:
-                nc.vector.tensor_tensor(out=dst, in0=pri, in1=acc[i, v][:], op=ALU.add)
-            seen[pair] += 1
-            rows_i = slice(P * i, P * (i + 1))
-            if pair in ((0, 0), (TILES - 1, VC // 2 - 1)):
-                nc.sync.dma_start(out=out[rows_i, NV * v : NV * (v + 1)], in_=dst)
-            elif seen[pair] == 2:
-                w0 = 2 * NV * (v // 2)
-                nc.sync.dma_start(out=out[rows_i, w0 : w0 + 2 * NV], in_=o[pair][:])
-
-        for g in range(KG2):
-            for k in range(KG1):
-                first_product(0, g, k)
-        for g in range(KG2):
-            for k in range(KG1):
-                first_product(1, g, k)
-        eng = {"v": nc.vector, "g": nc.gpsimd}
-        def run_item(it):
-            kind = it[0]
-            if kind == "s1":
-                for k in range(KG1):
-                    first_product(it[1], it[2], k)
-            if kind == "zc":
-                copy_z(it[1], it[2])
-            if kind == "soft":
-                i, g = it[1], it[2]
-                soft(i, g, zc[i, g] if (i, g) in zc else z[i, g], PC if i == 0 else 1)
-            if kind == "weigh":
-                weigh(eng[it[3]], it[1], it[2], PC if it[1] == 0 else 1)
-            if kind == "sig":
-                i, g = it[1], it[2]
-                sigmoid(i, g, zc[i, g] if (i, g) in zc else z[i, g])
-            if kind == "log":
-                log(it[1], it[2], PC if it[1] == 0 else 1)
-            if kind == "turn":
-                turn(it[1], it[2])
-            if kind == "group":
-                group(it[1], it[2], it[3] == "s")
-            if kind == "quant":
-                quantise(it[1], it[2] if it[1] == 0 else 0, it[2] + 1 if it[1] == 0 else 2)
-            if kind == "score":
-                multiply(it[1], it[2])
-            if kind == "evV":
-                leave(it[1] // 8, it[1] % 8, False)
-            if kind == "evS":
-                leave_raw(it[1] // 8, it[1] % 8)
-            if kind == "add":
-                leave(it[1] // 8, it[1] % 8, True)
-        for it in PLAN:
-            run_item(it)
+                finish(n, nc.vector, acc[n])
+            for step in after.get(n, []):
+                step()
+            if n - ADD_LATER in BY_SCALAR:
+                finish(n - ADD_LATER, nc.gpsimd, raw[n - ADD_LATER])

from contextlib import ExitStack

import concourse.mybir as mybir
from concourse.masks import make_identity

T, D, B, V = 512, 2048, 1024, 4096
FLOPS = 2 * T * D * B + 2 * T * B * V

F32 = mybir.dt.float32
BF16 = mybir.dt.bfloat16
I32 = mybir.dt.int32
U32 = mybir.dt.uint32
U8 = mybir.dt.uint8
E4M3X4 = mybir.dt.float8_e4m3fn_x4
E2M1X4 = mybir.dt.float4_e2m1fn_x4
ALU = mybir.AluOpType
ACT = mybir.ActivationFunctionType

P = 128
K_PASS = 512
BANK = 512
D_PASSES = D // K_PASS
GROUPS = B // K_PASS
TILES = T // P
CHUNKS = V // BANK
EPS = 2.0**-60

BY_SCALAR = (6, 9, 10, 18, 28)
ADD_LATER = 2


def tile_vocabulary_code_scores_s4_kernel(
    tc, hid_words, hid_scales, proj_words, proj_scales, code_words, code_scales, trust, prior, out
):
    nc = tc.nc
    with ExitStack() as ctx:
        keep = ctx.enter_context(tc.tile_pool(name="keep", bufs=1))
        work = ctx.enter_context(tc.tile_pool(name="work", bufs=4))
        outs = ctx.enter_context(tc.tile_pool(name="outs", bufs=6))
        psum = ctx.enter_context(tc.psum_pool(name="psum", bufs=8))
        ctx.enter_context(tc.manual_schedule())

        h_scales = keep.tile([P, D_PASSES, T], U8, name="h_scales", align_bytes=64)
        e_scales = keep.tile([P, D_PASSES, B], U8, name="e_scales", align_bytes=64)
        c_scales = keep.tile([P, V], U8, name="c_scales", align_bytes=64)
        rows = keep.tile([P, 32], F32, name="rows", align_bytes=64)
        warm = keep.tile([P, 1], F32, name="warm")
        nc.vector.memset(e_scales[:].rearrange("p g n -> p (g n)").bitcast(I32), 0)
        nc.vector.memset(h_scales[:].rearrange("p g n -> p (g n)").bitcast(I32), 0)
        nc.vector.memset(warm[:], 0.0)
        nc.vector.memset(rows[:], 0.0)

        h_words = [keep.tile([P, D_PASSES, T], U8, name=f"h_words{j}", align_bytes=64) for j in range(2)]
        e_words = [keep.tile([P, 2, 2 * B], U8, name=f"e_words{j}", align_bytes=64) for j in range(2)]

        def load_h_words(j):
            nc.sync.dma_start(
                out=h_words[j][:].bitcast(I32),
                in_=hid_words[:, :, T * j : T * (j + 1)].rearrange("g p n -> p g n").bitcast(I32),
            )

        for j in range(2):
            nc.gpsimd.dma_start(
                out=e_words[j][:].bitcast(I32),
                in_=proj_words[2 * j : 2 * j + 2].rearrange("g p n -> p g n").bitcast(I32),
            )
        ident = keep.tile([P, P], F32, name="ident", align_bytes=64)
        make_identity(nc, ident[:])
        nc.gpsimd.memset(c_scales[:].bitcast(I32), 0)
        load_h_words(0)
        for plane, source in ((e_scales, proj_scales), (h_scales, hid_scales)):
            for q in range(4):
                nc.sync.dma_start(
                    out=plane[32 * q : 32 * q + 4, :, :].bitcast(I32),
                    in_=source[:, 4 * q : 4 * q + 4, :].rearrange("g r n -> r g n").bitcast(I32),
                )
        load_h_words(1)
        nc.sync.dma_start(out=rows[0:64, :], in_=prior.rearrange("(c k) -> c k", k=64).bitcast(F32))
        nc.sync.dma_start(out=rows[64:80, :], in_=trust.rearrange("(c k) -> c k", k=64).bitcast(F32))
        c_words = []
        for j in range(CHUNKS // 2):
            words = keep.tile([P, GROUPS, 2 * BANK], U32, name=f"c_words{j}", align_bytes=64)
            nc.sync.dma_start(
                out=words[:].bitcast(I32),
                in_=code_words[:, :, 2 * BANK * j : 2 * BANK * (j + 1), :]
                .rearrange("g p n t -> p g (n t)")
                .bitcast(I32),
            )
            c_words.append(words)
            if j == 0:
                for q in range(4):
                    nc.sync.dma_start(
                        out=c_scales[32 * q : 32 * q + 8, :].bitcast(I32),
                        in_=code_scales[:, 4 * q : 4 * q + 4, :].bitcast(I32),
                    )
        nc.scalar.activation(out=warm[:], in_=warm[:], func=ACT.Sigmoid)

        z, s, ln, y, a, xt, grouped, codes, scales, acc, raw, pairs = ({} for n in range(12))

        def project(i, g):
            z[i, g] = psum.tile([P, K_PASS], F32, name="z", tag="bank")
            for k in range(D_PASSES):
                h0, e0 = 2 * P * (i % 2), 2 * K_PASS * g
                nc.tensor.matmul_mx(
                    out=z[i, g][:],
                    lhsT=h_words[i // 2][:, k, h0 : h0 + 2 * P].bitcast(E2M1X4),
                    lhsT_scale=h_scales[:, k, P * i : P * (i + 1)],
                    rhs=e_words[k // 2][:, k % 2, e0 : e0 + 2 * K_PASS].bitcast(E2M1X4),
                    rhs_scale=e_scales[:, k, K_PASS * g : K_PASS * (g + 1)],
                    start=(k == 0),
                    stop=(k == D_PASSES - 1),
                )

        def sigmoid(i, g):
            s[i, g] = work.tile([P, K_PASS], F32, name="s", tag="s")
            nc.scalar.activation(out=s[i, g][:], in_=z[i, g][:], func=ACT.Sigmoid)

        def log(i, g):
            ln[i, g] = work.tile([P, K_PASS], F32, name="ln", tag="ln")
            nc.scalar.activation(out=ln[i, g][:], in_=s[i, g][:], func=ACT.Ln, bias=EPS)

        def soften(i, g):
            y[i, g] = work.tile([P, K_PASS], F32, name="y", tag="y")
            nc.vector.tensor_tensor(out=y[i, g][:], in0=z[i, g][:], in1=ln[i, g][:], op=ALU.min)

        def weigh(engine, i, g):
            a[i, g] = work.tile([P, K_PASS], BF16, name="a", tag="a", align_bytes=64)
            engine.tensor_tensor(
                out=a[i, g][:], in0=y[i, g][:], in1=trust_b[:, K_PASS * g : K_PASS * (g + 1)], op=ALU.mult
            )

        def turn(i, g):
            words = a[i, g][:].bitcast(F32)
            xt[i, g] = psum.tile([P, 2, P], F32, name="xt", tag="bank")
            for u in range(2):
                nc.tensor.transpose(xt[i, g][:, u, :], words[:, u : K_PASS // 2 : 2], ident[:])

        def group(engine_copy, i, g):
            if i not in grouped:
                grouped[i] = work.tile([P, GROUPS, 4 * P], BF16, name="grouped", tag="grouped", align_bytes=64)
                codes[i] = keep.tile([P, GROUPS, P], U32, name=f"codes{i}", align_bytes=64)
                scales[i] = keep.tile([P, GROUPS, P], U8, name=f"scales{i}", align_bytes=64)
            engine_copy(
                out=grouped[i][:, g, :].bitcast(F32).rearrange("p (r u) -> p r u", u=2),
                in_=xt[i, g][:].rearrange("p u r -> p r u"),
            )

        def quantise(i, first, last):
            nc.vector.quantize_mx(
                out=codes[i][:, first : last + 1, :].rearrange("p g r -> p (g r)").bitcast(E4M3X4),
                scales=scales[i][:, first : last + 1, :].rearrange("p g r -> p (g r)"),
                in_=grouped[i][:, first : last + 1, :].rearrange("p g r -> p (g r)"),
            )

        def score(n):
            i, v = divmod(n, CHUNKS)
            acc[n] = psum.tile([P, BANK], F32, name="acc", tag="bank")
            c0 = BANK * (v % 2)
            for g in range(GROUPS):
                nc.tensor.matmul_mx(
                    out=acc[n][:],
                    lhsT=codes[i][:, g, :].bitcast(E4M3X4),
                    lhsT_scale=scales[i][:, g, :],
                    rhs=c_words[v // 2][:, g, c0 : c0 + BANK].bitcast(E4M3X4),
                    rhs_scale=c_scales[4 * g :, BANK * v : BANK * (v + 1)],
                    start=(g == 0),
                    stop=(g == GROUPS - 1),
                )

        def finish(n, engine, sums):
            i, v = divmod(n, CHUNKS)
            if n // 2 not in pairs:
                pairs[n // 2] = [outs.tile([P, 2 * BANK], F32, name="o", tag="o"), 0]
            o = pairs[n // 2][0]
            half = o[:, BANK * (v % 2) : BANK * (v % 2 + 1)]
            engine.tensor_tensor(out=half, in0=prior_b[:, BANK * v : BANK * (v + 1)], in1=sums[:], op=ALU.add)
            pairs[n // 2][1] += 1
            tokens = slice(P * i, P * (i + 1))
            if n // 2 in (0, TILES * CHUNKS // 2 - 1):
                nc.sync.dma_start(out=out[tokens, BANK * v : BANK * (v + 1)], in_=half)
            elif pairs[n // 2][1] == 2:
                v0 = v - v % 2
                nc.sync.dma_start(out=out[tokens, BANK * v0 : BANK * (v0 + 2)], in_=o[:])

        early = [(i, g) for i in (0, 1) for g in range(GROUPS)]
        late = [(i, g) for i in (2, 3) for g in range(GROUPS)]

        for g in range(GROUPS):
            project(0, g)

        rows4 = keep.tile([P, 4, 32], F32, name="rows4", align_bytes=64)
        cols = keep.tile([P, P], F32, name="cols", align_bytes=64)
        nc.vector.tensor_copy(out=rows4[:], in_=rows[:].unsqueeze(1).to_broadcast([P, 4, 32]))
        turned = psum.tile([P, P], F32, name="turned", tag="bank")
        nc.tensor.transpose(turned[:], rows4[:].rearrange("p a k -> p (a k)"), ident[:])
        nc.vector.tensor_copy(out=cols[:], in_=turned[:])

        def spread(name, first, count):
            repeated = keep.tile([P, count, 32], F32, name=f"{name}_repeated", align_bytes=64)
            words = keep.tile([P, 32 * count], F32, name=f"{name}_words", align_bytes=64)
            column = cols[:, first : first + count].unsqueeze(2)
            nc.vector.tensor_copy(out=repeated[:], in_=column.to_broadcast([P, count, 32]))
            nc.vector.transpose(out=words[:], in_=repeated[:].rearrange("p c m -> p (c m)"))
            return words[:].bitcast(BF16)

        for g in range(GROUPS):
            project(1, g)
        trust_b = spread("trust", 64, 16)
        prior_b = spread("prior", 0, 64)

        for i, g in early:
            sigmoid(i, g)
        for i, g in late:
            project(i, g)
        for i, g in early:
            log(i, g)
        soften(0, 0)
        soften(0, 1)
        weigh(nc.gpsimd, 0, 0)
        soften(1, 0)
        soften(1, 1)
        for i, g in late:
            sigmoid(i, g)
        weigh(nc.vector, 0, 1)
        turn(0, 0)
        turn(0, 1)
        weigh(nc.vector, 1, 0)
        group(nc.vector.tensor_copy, 0, 0)
        group(nc.vector.tensor_copy, 0, 1)
        weigh(nc.gpsimd, 1, 1)
        quantise(0, 0, 0)
        quantise(0, 1, 1)
        turn(1, 0)
        turn(1, 1)
        group(nc.vector.tensor_copy, 1, 0)
        group(nc.vector.tensor_copy, 1, 1)
        for i, g in late:
            log(i, g)

        def turn_and_group(i):
            for g in range(GROUPS):
                turn(i, g)
            for g in range(GROUPS):
                group(nc.scalar.copy, i, g)

        before = {
            0: [lambda: quantise(1, 0, 1)],
            3: [lambda: soften(2, 0)],
            5: [lambda: soften(2, 1)],
            10: [lambda: soften(3, 0)],
            11: [lambda: turn_and_group(2)],
            12: [lambda: quantise(2, 0, 1)],
            13: [lambda: soften(3, 1)],
            20: [lambda: turn_and_group(3)],
            21: [lambda: quantise(3, 0, 1)],
        }
        after = {
            3: [lambda: weigh(nc.gpsimd, 2, 0)],
            5: [lambda: weigh(nc.vector, 2, 1)],
            18: [lambda: weigh(nc.gpsimd, 3, 0), lambda: weigh(nc.gpsimd, 3, 1)],
        }
        for n in range(TILES * CHUNKS):
            score(n)
            for step in before.get(n, []):
                step()
            if n in BY_SCALAR:
                raw[n] = work.tile([P, BANK], F32, name="raw", tag="raw")
                nc.scalar.copy(out=raw[n][:], in_=acc[n][:])
            else:
                finish(n, nc.vector, acc[n])
            for step in after.get(n, []):
                step()
            if n - ADD_LATER in BY_SCALAR:
                finish(n - ADD_LATER, nc.gpsimd, raw[n - ADD_LATER])
